import numpy as np
import ml_dtypes


def mxq(x, axis, fmt="e4m3"):
    dtype, down = {"e4m3": (ml_dtypes.float8_e4m3fn, 7), "e5m2": (ml_dtypes.float8_e5m2, 14)}[fmt]
    v = np.moveaxis(np.asarray(x, np.float32).astype(ml_dtypes.bfloat16).astype(np.float64), axis, -1)
    blocks = v.reshape(v.shape[:-1] + (-1, 32))
    amax = np.abs(blocks).max(-1, keepdims=True)
    byte = np.maximum(np.where(amax > 0, np.frexp(amax)[1] - 1 + 127, 0) - down, 1)
    scale = np.exp2(byte - 127.0)
    codes = (blocks / scale).astype(np.float32).astype(dtype).astype(np.float64)
    return np.moveaxis((codes * scale).reshape(v.shape), -1, axis)


WIDE = False


def mx_kscale(k):
    if not WIDE:
        return np.ones(k)
    levels = np.array([10, -10, 5, -5, 0])
    if k % 512:
        return np.exp2(np.random.permutation(np.resize(levels, k // 32))).repeat(32)
    a = np.empty((k // 512, 16))
    for p in range(k // 512):
        a[p, :8] = np.random.permutation(np.resize(levels, 8))
        for g in range(8):
            far = levels[np.abs(levels - a[p, g]) >= 10]
            a[p, g + 8] = far[np.random.randint(len(far))]
    return np.exp2(a.ravel()).repeat(32)


def f64(x):
    return np.asarray(x).astype(np.float64)


def striped(idx):
    return np.tile(idx.reshape(-1, 16).T, (8, 1)).astype(np.uint16)


def unstriped(offs):
    return offs[:16].T.reshape(-1).astype(np.int64)


def pack_weight(w):
    k, n = w.shape
    w = f64(np.asarray(w, np.float32).astype(ml_dtypes.bfloat16)).reshape(k // 32, 32, n)
    amax = np.abs(w).max(1)
    byte = np.clip(np.where(amax > 0, np.frexp(amax)[1] - 1 + 127 - 7, 1), 1, 254)
    scaled = (w * np.exp2(127.0 - byte)[:, None, :]).reshape(k, n).astype(np.float32)
    words = np.ascontiguousarray(scaled.reshape(k // 512, 128, 4, n).transpose(0, 1, 3, 2)).astype(ml_dtypes.float8_e4m3fn).view(np.uint8)
    return words, np.ascontiguousarray(byte.astype(np.uint8).reshape(k // 512, 16, n))


def unpack_weight(words, scales):
    g, p, n, _ = words.shape
    vals = np.ascontiguousarray(words).view(ml_dtypes.float8_e4m3fn).astype(np.float64) * np.repeat(np.exp2(scales.astype(np.float64) - 127.0), 8, axis=1)[..., None]
    return vals.transpose(0, 1, 3, 2).reshape(g * 512, n)


def gelu(v):
    return 0.5 * v * (1.0 + np.tanh(np.sqrt(2.0 / np.pi) * (v + 0.044715 * v**3)))


K, T, D, S, V, N = 1024, 1024, 16, 512, 32, 128


def setup_inputs():
    n = np.random.standard_normal
    s = mx_kscale(K)[:, None]
    words, scales = pack_weight(n((K, N)) / np.sqrt(K) / s)
    return {
        "xT": (n((K, T)) * s).astype(np.float32),
        "w_words": words,
        "w_scales": scales,
        "b": (0.3 * n((N, 1))).astype(np.float32),
        "offs": striped(np.random.permutation(T)[:S]),
    }


def reference(xT, w_words, w_scales, b, offs):
    w = unpack_weight(w_words, w_scales)
    idx = unstriped(offs)
    xq = mxq(f64(xT)[:, idx], 0, "e4m3")
    y = w.T @ xq
    y = gelu(y + f64(b))
    return y.reshape(N, V, D).max(axis=2)

@@ -1,0 +1,139 @@
+from contextlib import ExitStack
+
+import concourse.mybir as mybir
+
+K, T, S, D, N = 1024, 1024, 512, 16, 128
+FLOPS = 2 * K * S * N
+
+F32 = mybir.dt.float32
+BF16 = mybir.dt.bfloat16
+U32 = mybir.dt.uint32
+I32 = mybir.dt.int32
+U16 = mybir.dt.uint16
+U8 = mybir.dt.uint8
+FP8X4 = mybir.dt.float8_e4m3fn_x4
+GELU = mybir.ActivationFunctionType.Gelu_apprx_tanh
+
+P = 128
+SLICE = 128
+CHUNKS = (
+    ((768, 512), (256, 160)),
+    ((512, 0), (512, 352)),
+    ((512, 0), (512, 352)),
+    ((512, 0), (256, 256), (256, 112)),
+)
+W_AFTER = 5
+
+
+def tile_picked_pool_lin_gelu_sub_e_kernel(tc, xT, w_words, w_scales, b, offs, out):
+    nc = tc.nc
+    with ExitStack() as ctx:
+        keep = ctx.enter_context(tc.tile_pool(name="keep", bufs=1))
+        psum = ctx.enter_context(tc.psum_pool(name="psum", bufs=1))
+
+        offsets = keep.tile([P, S // 16], U16, name="offsets")
+        w_codes = keep.tile([P, 2, N], U32, name="w_codes", align_bytes=64)
+        w_plane = keep.tile([P, 2, N], U8, name="w_plane", align_bytes=64)
+        bias = keep.tile([P, 1], F32, name="bias")
+        warm = keep.tile([P, 2], F32, name="warm")
+
+        rows = xT.rearrange("(a p u e) t -> a u p e t", a=2, p=P, u=2, e=2)
+        raw = {}
+        count = 0
+        for j, chunks in enumerate(CHUNKS):
+            c0 = 0
+            for c, (width, share) in enumerate(chunks):
+                raw[j, c] = keep.tile([P, 2, width], F32, name="raw%d_%d" % (j, c))
+                nc.sync.dma_start(out=raw[j, c][:], in_=rows[j // 2, j % 2][:, :, c0 : c0 + width])
+                c0 += width
+                count += 1
+                if count == 1:
+                    nc.sync.dma_start(offsets[:], offs)
+                if count == W_AFTER:
+                    nc.sync.dma_start(
+                        out=w_codes[:].bitcast(I32),
+                        in_=w_words.rearrange("a p m r -> p a (m r)").bitcast(I32),
+                    )
+
+        nc.vector.memset(warm[:, 0:1], 0.0)
+        nc.scalar.activation(warm[:, 1:2], warm[:, 0:1], GELU)
+
+        nc.gpsimd.memset(w_plane[:], 0)
+        scale_rows = w_scales.rearrange("a q m -> q a m")
+        for q in range(4):
+            nc.gpsimd.dma_start(
+                out=w_plane[32 * q : 32 * q + 4].bitcast(I32),
+                in_=scale_rows[4 * q : 4 * q + 4].bitcast(I32),
+            )
+        nc.gpsimd.dma_start(out=bias[:], in_=b)
+
+        def round_pair(j):
+            pairs = keep.tile([P, T, 2], BF16, name="pairs%d" % j)
+            c0 = 0
+            for c, (width, share) in enumerate(CHUNKS[j]):
+                src = raw[j, c][:].rearrange("p e t -> p t e")
+                if share > 0:
+                    nc.vector.tensor_copy(out=pairs[:, c0 : c0 + share, :], in_=src[:, 0:share, :])
+                if share < width:
+                    nc.scalar.copy(out=pairs[:, c0 + share : c0 + width, :], in_=src[:, share:width, :])
+                c0 += width
+            return pairs[:].rearrange("p t e -> p (t e)").bitcast(U32)
+
+        picked = [keep.tile([P, S * 4], BF16, name="picked%d" % a, align_bytes=64) for a in range(2)]
+        codes = [keep.tile([P, S], U32, name="codes%d" % a, align_bytes=64) for a in range(2)]
+        plane = [keep.tile([P, S], U8, name="plane%d" % a, align_bytes=64) for a in range(2)]
+        halves = keep.tile([P, 2, S * 2], BF16, name="halves")
+        acc = [psum.tile([P, SLICE], F32, name="acc%d" % s) for s in range(S // SLICE)]
+        act = keep.tile([P, S], F32, name="act")
+        pooled = keep.tile([P, S // D], F32, name="pooled")
+
+        def multiply(a, s):
+            cols = slice(s * SLICE, (s + 1) * SLICE)
+            nc.tensor.matmul_mx(
+                out=acc[s][:],
+                lhsT=w_codes[:, a, :].bitcast(FP8X4),
+                lhsT_scale=w_plane[:, a, :],
+                rhs=codes[a][:, cols].bitcast(FP8X4),
+                rhs_scale=plane[a][:, cols],
+                start=(a == 0),
+                stop=(a == 1),
+            )
+
+        words0 = picked[0][:].bitcast(U32).rearrange("p (n u) -> p n u", u=2)
+        for u in range(2):
+            window = round_pair(u)
+            nc.vector.tensor_copy(words0[:, :, u], window.indirect(offsets[:]))
+        window2 = round_pair(2)
+        nc.vector.quantize_mx(out=codes[0][:].bitcast(FP8X4), scales=plane[0][:], in_=picked[0][:])
+        for s in range(S // SLICE):
+            multiply(0, s)
+
+        half_words = halves[:].bitcast(U32)
+        words1 = picked[1][:].bitcast(U32).rearrange("p (n u) -> p n u", u=2)
+        nc.vector.tensor_copy(half_words[:, 0, :], window2.indirect(offsets[:]))
+        window3 = round_pair(3)
+        for s in range(S // SLICE):
+            cols = slice(s * SLICE, (s + 1) * SLICE)
+            lists = offsets[:, s * SLICE // 16 : (s + 1) * SLICE // 16]
+            nc.vector.tensor_copy(half_words[:, 1, cols], window3.indirect(lists))
+        for s in range(S // SLICE):
+            cols = slice(s * SLICE, (s + 1) * SLICE)
+            nc.scalar.copy(out=words1[:, cols, :], in_=half_words[:, :, cols].rearrange("p u n -> p n u"))
+        for s in range(S // SLICE):
+            cols = slice(s * SLICE, (s + 1) * SLICE)
+            nc.vector.quantize_mx(
+                out=codes[1][:, cols].bitcast(FP8X4),
+                scales=plane[1][:, cols],
+                in_=picked[1][:, 4 * s * SLICE : 4 * (s + 1) * SLICE],
+            )
+            multiply(1, s)
+        for s in range(S // SLICE):
+            cols = slice(s * SLICE, (s + 1) * SLICE)
+            nc.scalar.activation(act[:, cols], acc[s][:], GELU, bias=bias[:])
+            nc.vector.tensor_reduce(
+                out=pooled[:, s * SLICE // D : (s + 1) * SLICE // D],
+                in_=act[:, cols].rearrange("p (v d) -> p v d", d=D),
+                axis=mybir.AxisListType.X,
+                op=mybir.AluOpType.max,
+            )
+        nc.sync.dma_start(out=out, in_=pooled[:])

@@ -15,14 +15,13 @@ FP8X4 = mybir.dt.float8_e4m3fn_x4
 GELU = mybir.ActivationFunctionType.Gelu_apprx_tanh
 
 P = 128
+PER_COLUMN = 16
+HALF_T = T // 2
+HALF_S = S // 2
 SLICE = 128
-CHUNKS = (
-    ((768, 512), (256, 160)),
-    ((512, 0), (512, 352)),
-    ((512, 0), (512, 352)),
-    ((512, 0), (256, 256), (256, 112)),
-)
-W_AFTER = 5
+SLICES = S // SLICE
+
+VECTOR_NODES = {(0, 1): 304, (1, 0): 144, (1, 1): 288}
 
 
 def tile_picked_pool_lin_gelu_sub_e_kernel(tc, xT, w_words, w_scales, b, offs, out):
@@ -31,103 +30,105 @@ def tile_picked_pool_lin_gelu_sub_e_kernel(tc, xT, w_words, w_scales, b, offs, o
         keep = ctx.enter_context(tc.tile_pool(name="keep", bufs=1))
         psum = ctx.enter_context(tc.psum_pool(name="psum", bufs=1))
 
-        offsets = keep.tile([P, S // 16], U16, name="offsets")
-        w_codes = keep.tile([P, 2, N], U32, name="w_codes", align_bytes=64)
-        w_plane = keep.tile([P, 2, N], U8, name="w_plane", align_bytes=64)
-        bias = keep.tile([P, 1], F32, name="bias")
-        warm = keep.tile([P, 2], F32, name="warm")
-
+        offsets = keep.tile([P, S // PER_COLUMN], U16, name="offsets")
+        nc.sync.dma_start(offsets[:], offs)
         rows = xT.rearrange("(a p u e) t -> a u p e t", a=2, p=P, u=2, e=2)
+        first_planes = [keep.tile([P, T], F32, name="first_plane%d" % e) for e in range(2)]
+        for e in range(2):
+            nc.sync.dma_start(out=first_planes[e][:], in_=rows[0, 0][:, e, :])
         raw = {}
-        count = 0
-        for j, chunks in enumerate(CHUNKS):
-            c0 = 0
-            for c, (width, share) in enumerate(chunks):
-                raw[j, c] = keep.tile([P, 2, width], F32, name="raw%d_%d" % (j, c))
-                nc.sync.dma_start(out=raw[j, c][:], in_=rows[j // 2, j % 2][:, :, c0 : c0 + width])
-                c0 += width
-                count += 1
-                if count == 1:
-                    nc.sync.dma_start(offsets[:], offs)
-                if count == W_AFTER:
-                    nc.sync.dma_start(
-                        out=w_codes[:].bitcast(I32),
-                        in_=w_words.rearrange("a p m r -> p a (m r)").bitcast(I32),
-                    )
+        for a, u in VECTOR_NODES:
+            for h in range(2):
+                raw[a, u, h] = keep.tile([P, 2, HALF_T], F32, name="raw%d%d%d" % (a, u, h))
+                nc.sync.dma_start(out=raw[a, u, h][:], in_=rows[a, u][:, :, h * HALF_T : (h + 1) * HALF_T])
 
+        w_codes = keep.tile([P, 2, N], U32, name="w_codes", align_bytes=64)
+        nc.sync.dma_start(
+            out=w_codes[:].bitcast(I32),
+            in_=w_words.rearrange("a p m r -> p a (m r)").bitcast(I32),
+        )
+        w_scale_bytes = keep.tile([P, 2, N], U8, name="w_scale_bytes", align_bytes=64)
+        nc.vector.memset(w_scale_bytes[:].bitcast(I32), 0)
+        scale_rows = w_scales.rearrange("a q m -> q a m")
+        for q in range(4):
+            nc.sync.dma_start(
+                out=w_scale_bytes[32 * q : 32 * q + 4].bitcast(I32),
+                in_=scale_rows[4 * q : 4 * q + 4].bitcast(I32),
+            )
+        bias = keep.tile([P, 1], F32, name="bias")
+        nc.sync.dma_start(out=bias[:], in_=b)
+
+        warm = keep.tile([P, 2], F32, name="warm")
         nc.vector.memset(warm[:, 0:1], 0.0)
         nc.scalar.activation(warm[:, 1:2], warm[:, 0:1], GELU)
 
-        nc.gpsimd.memset(w_plane[:], 0)
-        scale_rows = w_scales.rearrange("a q m -> q a m")
-        for q in range(4):
-            nc.gpsimd.dma_start(
-                out=w_plane[32 * q : 32 * q + 4].bitcast(I32),
-                in_=scale_rows[4 * q : 4 * q + 4].bitcast(I32),
-            )
-        nc.gpsimd.dma_start(out=bias[:], in_=b)
-
-        def round_pair(j):
-            pairs = keep.tile([P, T, 2], BF16, name="pairs%d" % j)
-            c0 = 0
-            for c, (width, share) in enumerate(CHUNKS[j]):
-                src = raw[j, c][:].rearrange("p e t -> p t e")
-                if share > 0:
-                    nc.vector.tensor_copy(out=pairs[:, c0 : c0 + share, :], in_=src[:, 0:share, :])
-                if share < width:
-                    nc.scalar.copy(out=pairs[:, c0 + share : c0 + width, :], in_=src[:, share:width, :])
-                c0 += width
-            return pairs[:].rearrange("p t e -> p (t e)").bitcast(U32)
-
         picked = [keep.tile([P, S * 4], BF16, name="picked%d" % a, align_bytes=64) for a in range(2)]
         codes = [keep.tile([P, S], U32, name="codes%d" % a, align_bytes=64) for a in range(2)]
-        plane = [keep.tile([P, S], U8, name="plane%d" % a, align_bytes=64) for a in range(2)]
-        halves = keep.tile([P, 2, S * 2], BF16, name="halves")
-        acc = [psum.tile([P, SLICE], F32, name="acc%d" % s) for s in range(S // SLICE)]
+        scale_bytes = [keep.tile([P, S], U8, name="scale_bytes%d" % a, align_bytes=64) for a in range(2)]
+        picked_pairs = keep.tile([P, 2, S * 2], BF16, name="picked_pairs")
+        acc = [psum.tile([P, SLICE], F32, name="acc%d" % s) for s in range(SLICES)]
         act = keep.tile([P, S], F32, name="act")
         pooled = keep.tile([P, S // D], F32, name="pooled")
+
+        def round_pair(a, u):
+            pairs = keep.tile([P, T, 2], BF16, name="pairs%d%d" % (a, u))
+            nc.scalar.copy(out=pairs[:, 0:HALF_T, :], in_=raw[a, u, 0][:].rearrange("p e t -> p t e"))
+            second = raw[a, u, 1][:].rearrange("p e t -> p t e")
+            share = VECTOR_NODES[a, u]
+            nc.vector.tensor_copy(out=pairs[:, HALF_T : HALF_T + share, :], in_=second[:, 0:share, :])
+            nc.scalar.copy(out=pairs[:, HALF_T + share : T, :], in_=second[:, share:HALF_T, :])
+            return pairs[:].rearrange("p t e -> p (t e)").bitcast(U32)
+
+        def entries(lo, hi):
+            return offsets[:, lo // PER_COLUMN : hi // PER_COLUMN]
+
+        def quantize(a, lo, hi):
+            nc.vector.quantize_mx(
+                out=codes[a][:, lo:hi].bitcast(FP8X4),
+                scales=scale_bytes[a][:, lo:hi],
+                in_=picked[a][:, 4 * lo : 4 * hi],
+            )
 
         def multiply(a, s):
             cols = slice(s * SLICE, (s + 1) * SLICE)
             nc.tensor.matmul_mx(
                 out=acc[s][:],
                 lhsT=w_codes[:, a, :].bitcast(FP8X4),
-                lhsT_scale=w_plane[:, a, :],
+                lhsT_scale=w_scale_bytes[:, a, :],
                 rhs=codes[a][:, cols].bitcast(FP8X4),
-                rhs_scale=plane[a][:, cols],
+                rhs_scale=scale_bytes[a][:, cols],
                 start=(a == 0),
                 stop=(a == 1),
             )
 
+        values0 = picked[0][:].rearrange("p (n t) -> p n t", t=4)
+        for e in range(2):
+            nc.vector.tensor_copy(values0[:, :, e], first_planes[e][:].indirect(offsets[:]))
         words0 = picked[0][:].bitcast(U32).rearrange("p (n u) -> p n u", u=2)
-        for u in range(2):
-            window = round_pair(u)
-            nc.vector.tensor_copy(words0[:, :, u], window.indirect(offsets[:]))
-        window2 = round_pair(2)
-        nc.vector.quantize_mx(out=codes[0][:].bitcast(FP8X4), scales=plane[0][:], in_=picked[0][:])
-        for s in range(S // SLICE):
-            multiply(0, s)
+        window01 = round_pair(0, 1)
+        for lo in (0, HALF_S):
+            nc.vector.tensor_copy(words0[:, lo : lo + HALF_S, 1], window01.indirect(entries(lo, lo + HALF_S)))
+        window10 = round_pair(1, 0)
+        for lo in (0, HALF_S):
+            quantize(0, lo, lo + HALF_S)
 
-        half_words = halves[:].bitcast(U32)
+        pair_words = picked_pairs[:].bitcast(U32)
         words1 = picked[1][:].bitcast(U32).rearrange("p (n u) -> p n u", u=2)
-        nc.vector.tensor_copy(half_words[:, 0, :], window2.indirect(offsets[:]))
-        window3 = round_pair(3)
-        for s in range(S // SLICE):
+        nc.vector.tensor_copy(pair_words[:, 0, :], window10.indirect(offsets[:]))
+        window11 = round_pair(1, 1)
+        for s in range(SLICES):
+            multiply(0, s)
+        for s in range(SLICES):
+            lo = s * SLICE
+            nc.vector.tensor_copy(pair_words[:, 1, lo : lo + SLICE], window11.indirect(entries(lo, lo + SLICE)))
+        for s in range(SLICES):
             cols = slice(s * SLICE, (s + 1) * SLICE)
-            lists = offsets[:, s * SLICE // 16 : (s + 1) * SLICE // 16]
-            nc.vector.tensor_copy(half_words[:, 1, cols], window3.indirect(lists))
-        for s in range(S // SLICE):
-            cols = slice(s * SLICE, (s + 1) * SLICE)
-            nc.scalar.copy(out=words1[:, cols, :], in_=half_words[:, :, cols].rearrange("p u n -> p n u"))
-        for s in range(S // SLICE):
-            cols = slice(s * SLICE, (s + 1) * SLICE)
-            nc.vector.quantize_mx(
-                out=codes[1][:, cols].bitcast(FP8X4),
-                scales=plane[1][:, cols],
-                in_=picked[1][:, 4 * s * SLICE : 4 * (s + 1) * SLICE],
-            )
+            nc.scalar.copy(out=words1[:, cols, :], in_=pair_words[:, :, cols].rearrange("p u n -> p n u"))
+        for s in range(SLICES):
+            quantize(1, s * SLICE, (s + 1) * SLICE)
             multiply(1, s)
-        for s in range(S // SLICE):
+
+        for s in range(SLICES):
             cols = slice(s * SLICE, (s + 1) * SLICE)
             nc.scalar.activation(act[:, cols], acc[s][:], GELU, bias=bias[:])
             nc.vector.tensor_reduce(

@@ -21,7 +21,7 @@ HALF_S = S // 2
 SLICE = 128
 SLICES = S // SLICE
 
-VECTOR_NODES = {(0, 1): 304, (1, 0): 144, (1, 1): 288}
+VECTOR_NODES = {(0, 1): 304, (1, 0): 208, (1, 1): 320}
 
 
 def tile_picked_pool_lin_gelu_sub_e_kernel(tc, xT, w_words, w_scales, b, offs, out):
@@ -31,11 +31,12 @@ def tile_picked_pool_lin_gelu_sub_e_kernel(tc, xT, w_words, w_scales, b, offs, o
         psum = ctx.enter_context(tc.psum_pool(name="psum", bufs=1))
 
         offsets = keep.tile([P, S // PER_COLUMN], U16, name="offsets")
-        nc.sync.dma_start(offsets[:], offs)
         rows = xT.rearrange("(a p u e) t -> a u p e t", a=2, p=P, u=2, e=2)
         first_planes = [keep.tile([P, T], F32, name="first_plane%d" % e) for e in range(2)]
         for e in range(2):
             nc.sync.dma_start(out=first_planes[e][:], in_=rows[0, 0][:, e, :])
+            if e == 0:
+                nc.sync.dma_start(offsets[:], offs)
         raw = {}
         for a, u in VECTOR_NODES:
             for h in range(2):

from contextlib import ExitStack

import concourse.mybir as mybir

K, T, S, D, N = 1024, 1024, 512, 16, 128
FLOPS = 2 * K * S * N

F32 = mybir.dt.float32
BF16 = mybir.dt.bfloat16
U32 = mybir.dt.uint32
I32 = mybir.dt.int32
U16 = mybir.dt.uint16
U8 = mybir.dt.uint8
FP8X4 = mybir.dt.float8_e4m3fn_x4
GELU = mybir.ActivationFunctionType.Gelu_apprx_tanh

P = 128
PER_COLUMN = 16
HALF_T = T // 2
HALF_S = S // 2
SLICE = 128
SLICES = S // SLICE

VECTOR_NODES = {(0, 1): 304, (1, 0): 208, (1, 1): 320}


def tile_picked_pool_lin_gelu_sub_e_kernel(tc, xT, w_words, w_scales, b, offs, out):
    nc = tc.nc
    with ExitStack() as ctx:
        keep = ctx.enter_context(tc.tile_pool(name="keep", bufs=1))
        psum = ctx.enter_context(tc.psum_pool(name="psum", bufs=1))

        offsets = keep.tile([P, S // PER_COLUMN], U16, name="offsets")
        rows = xT.rearrange("(a p u e) t -> a u p e t", a=2, p=P, u=2, e=2)
        first_planes = [keep.tile([P, T], F32, name="first_plane%d" % e) for e in range(2)]
        for e in range(2):
            nc.sync.dma_start(out=first_planes[e][:], in_=rows[0, 0][:, e, :])
            if e == 0:
                nc.sync.dma_start(offsets[:], offs)
        raw = {}
        for a, u in VECTOR_NODES:
            for h in range(2):
                raw[a, u, h] = keep.tile([P, 2, HALF_T], F32, name="raw%d%d%d" % (a, u, h))
                nc.sync.dma_start(out=raw[a, u, h][:], in_=rows[a, u][:, :, h * HALF_T : (h + 1) * HALF_T])

        w_codes = keep.tile([P, 2, N], U32, name="w_codes", align_bytes=64)
        nc.sync.dma_start(
            out=w_codes[:].bitcast(I32),
            in_=w_words.rearrange("a p m r -> p a (m r)").bitcast(I32),
        )
        w_scale_bytes = keep.tile([P, 2, N], U8, name="w_scale_bytes", align_bytes=64)
        nc.vector.memset(w_scale_bytes[:].bitcast(I32), 0)
        scale_rows = w_scales.rearrange("a q m -> q a m")
        for q in range(4):
            nc.sync.dma_start(
                out=w_scale_bytes[32 * q : 32 * q + 4].bitcast(I32),
                in_=scale_rows[4 * q : 4 * q + 4].bitcast(I32),
            )
        bias = keep.tile([P, 1], F32, name="bias")
        nc.sync.dma_start(out=bias[:], in_=b)

        warm = keep.tile([P, 2], F32, name="warm")
        nc.vector.memset(warm[:, 0:1], 0.0)
        nc.scalar.activation(warm[:, 1:2], warm[:, 0:1], GELU)

        picked = [keep.tile([P, S * 4], BF16, name="picked%d" % a, align_bytes=64) for a in range(2)]
        codes = [keep.tile([P, S], U32, name="codes%d" % a, align_bytes=64) for a in range(2)]
        scale_bytes = [keep.tile([P, S], U8, name="scale_bytes%d" % a, align_bytes=64) for a in range(2)]
        picked_pairs = keep.tile([P, 2, S * 2], BF16, name="picked_pairs")
        acc = [psum.tile([P, SLICE], F32, name="acc%d" % s) for s in range(SLICES)]
        act = keep.tile([P, S], F32, name="act")
        pooled = keep.tile([P, S // D], F32, name="pooled")

        def round_pair(a, u):
            pairs = keep.tile([P, T, 2], BF16, name="pairs%d%d" % (a, u))
            nc.scalar.copy(out=pairs[:, 0:HALF_T, :], in_=raw[a, u, 0][:].rearrange("p e t -> p t e"))
            second = raw[a, u, 1][:].rearrange("p e t -> p t e")
            share = VECTOR_NODES[a, u]
            nc.vector.tensor_copy(out=pairs[:, HALF_T : HALF_T + share, :], in_=second[:, 0:share, :])
            nc.scalar.copy(out=pairs[:, HALF_T + share : T, :], in_=second[:, share:HALF_T, :])
            return pairs[:].rearrange("p t e -> p (t e)").bitcast(U32)

        def entries(lo, hi):
            return offsets[:, lo // PER_COLUMN : hi // PER_COLUMN]

        def quantize(a, lo, hi):
            nc.vector.quantize_mx(
                out=codes[a][:, lo:hi].bitcast(FP8X4),
                scales=scale_bytes[a][:, lo:hi],
                in_=picked[a][:, 4 * lo : 4 * hi],
            )

        def multiply(a, s):
            cols = slice(s * SLICE, (s + 1) * SLICE)
            nc.tensor.matmul_mx(
                out=acc[s][:],
                lhsT=w_codes[:, a, :].bitcast(FP8X4),
                lhsT_scale=w_scale_bytes[:, a, :],
                rhs=codes[a][:, cols].bitcast(FP8X4),
                rhs_scale=scale_bytes[a][:, cols],
                start=(a == 0),
                stop=(a == 1),
            )

        values0 = picked[0][:].rearrange("p (n t) -> p n t", t=4)
        for e in range(2):
            nc.vector.tensor_copy(values0[:, :, e], first_planes[e][:].indirect(offsets[:]))
        words0 = picked[0][:].bitcast(U32).rearrange("p (n u) -> p n u", u=2)
        window01 = round_pair(0, 1)
        for lo in (0, HALF_S):
            nc.vector.tensor_copy(words0[:, lo : lo + HALF_S, 1], window01.indirect(entries(lo, lo + HALF_S)))
        window10 = round_pair(1, 0)
        for lo in (0, HALF_S):
            quantize(0, lo, lo + HALF_S)

        pair_words = picked_pairs[:].bitcast(U32)
        words1 = picked[1][:].bitcast(U32).rearrange("p (n u) -> p n u", u=2)
        nc.vector.tensor_copy(pair_words[:, 0, :], window10.indirect(offsets[:]))
        window11 = round_pair(1, 1)
        for s in range(SLICES):
            multiply(0, s)
        for s in range(SLICES):
            lo = s * SLICE
            nc.vector.tensor_copy(pair_words[:, 1, lo : lo + SLICE], window11.indirect(entries(lo, lo + SLICE)))
        for s in range(SLICES):
            cols = slice(s * SLICE, (s + 1) * SLICE)
            nc.scalar.copy(out=words1[:, cols, :], in_=pair_words[:, :, cols].rearrange("p u n -> p n u"))
        for s in range(SLICES):
            quantize(1, s * SLICE, (s + 1) * SLICE)
            multiply(1, s)

        for s in range(SLICES):
            cols = slice(s * SLICE, (s + 1) * SLICE)
            nc.scalar.activation(act[:, cols], acc[s][:], GELU, bias=bias[:])
            nc.vector.tensor_reduce(
                out=pooled[:, s * SLICE // D : (s + 1) * SLICE // D],
                in_=act[:, cols].rearrange("p (v d) -> p v d", d=D),
                axis=mybir.AxisListType.X,
                op=mybir.AluOpType.max,
            )
        nc.sync.dma_start(out=out, in_=pooled[:])
